import numpy as np
import ml_dtypes


def mxq(x, axis, fmt="e4m3"):
    dtype, down = {"e4m3": (ml_dtypes.float8_e4m3fn, 7), "e5m2": (ml_dtypes.float8_e5m2, 14)}[fmt]
    v = np.moveaxis(np.asarray(x, np.float32).astype(ml_dtypes.bfloat16).astype(np.float64), axis, -1)
    blocks = v.reshape(v.shape[:-1] + (-1, 32))
    amax = np.abs(blocks).max(-1, keepdims=True)
    byte = np.maximum(np.where(amax > 0, np.frexp(amax)[1] - 1 + 127, 0) - down, 1)
    scale = np.exp2(byte - 127.0)
    codes = (blocks / scale).astype(np.float32).astype(dtype).astype(np.float64)
    return np.moveaxis((codes * scale).reshape(v.shape), -1, axis)


WIDE = False


def mx_kscale(k):
    if not WIDE:
        return np.ones(k)
    levels = np.array([10, -10, 5, -5, 0])
    if k % 512:
        return np.exp2(np.random.permutation(np.resize(levels, k // 32))).repeat(32)
    a = np.empty((k // 512, 16))
    for p in range(k // 512):
        a[p, :8] = np.random.permutation(np.resize(levels, 8))
        for g in range(8):
            far = levels[np.abs(levels - a[p, g]) >= 10]
            a[p, g + 8] = far[np.random.randint(len(far))]
    return np.exp2(a.ravel()).repeat(32)


BF16 = ml_dtypes.bfloat16


def bf(x):
    return np.asarray(x, np.float32).astype(BF16)


def f64(x):
    return np.asarray(x).astype(np.float64)


E2M1 = np.array([0.0, 0.5, 1.0, 1.5, 2.0, 3.0, 4.0, 6.0, -0.0, -0.5, -1.0, -1.5, -2.0, -3.0, -4.0, -6.0])


def pack_weight(w, fmt):
    k, n = w.shape
    w = f64(bf(w)).reshape(k // 32, 32, n)
    amax = np.abs(w).max(1)
    if fmt == "e4m3":
        byte = np.frexp(amax)[1] - 1 + 127 - 7
    else:
        mant, ex = np.frexp(amax / 6.0)
        byte = np.where(mant > 0.5, ex, ex - 1) + 127
    byte = np.clip(np.where(amax > 0, byte, 1), 1, 254)
    scaled = (w * np.exp2(127.0 - byte)[:, None, :]).reshape(k, n).astype(np.float32)
    by_word = np.ascontiguousarray(scaled.reshape(k // 512, 128, 4, n).transpose(0, 1, 3, 2))
    if fmt == "e4m3":
        words = by_word.astype(ml_dtypes.float8_e4m3fn).view(np.uint8)
    else:
        c = by_word.astype(ml_dtypes.float4_e2m1fn).view(np.uint8) & 0xF
        words = c[..., 0::2] | (c[..., 1::2] << 4)
    return np.ascontiguousarray(words), np.ascontiguousarray(byte.astype(np.uint8).reshape(k // 512, 16, n))


def unpack_weight(words, scales, fmt):
    g, p, n, _ = words.shape
    if fmt == "e4m3":
        vals = np.ascontiguousarray(words).view(ml_dtypes.float8_e4m3fn).astype(np.float64)
    else:
        nib = np.empty((g, p, n, 4), np.uint8)
        nib[..., 0::2] = words & 0xF
        nib[..., 1::2] = words >> 4
        vals = E2M1[nib]
    vals = vals * np.repeat(np.exp2(scales.astype(np.float64) - 127.0), 8, axis=1)[..., None]
    return vals.transpose(0, 1, 3, 2).reshape(g * 512, n)
def pack4(w):
    words, scales = pack_weight(w, "e2m1")
    return words.reshape(words.shape[0], 128, -1), scales


def unpack4(words, scales):
    return unpack_weight(words.reshape(words.shape[0], 128, -1, 2), scales, "e2m1")


P, K, J, T, R = 2048, 512, 1024, 512, 512


def draw0():
    s, t, u = mx_kscale(K), mx_kscale(J), mx_kscale(P)
    effects = np.random.standard_normal((J, T)) / np.sqrt(J) / t[:, None]
    effects_words, effects_scales = pack4(effects)
    return {"windows": bf(np.random.standard_normal((P, K)) * s),
            "motifs": bf(2.0 * np.random.standard_normal((K, J)) / np.sqrt(K) / s[:, None]),
            "access": bf(np.random.uniform(0.3, 1.7, P) * u),
            "activity": bf(np.random.uniform(0.5, 1.5, J) * t),
            "effects_words": effects_words,
            "effects_scales": effects_scales,
            "pool": bf(np.random.standard_normal((R, P)) / np.sqrt(P) / u)}


def core(windows, motifs, access, activity, effects_words, effects_scales, pool):
    score = mxq(f64(windows), 1, "e4m3") @ mxq(f64(motifs), 0, "e4m3")
    occ = 1.0 / (1.0 + np.exp(-score)) * f64(access)[:, None] * f64(activity)
    track = mxq(occ, 1, "e4m3") @ unpack4(effects_words, effects_scales)
    load = mxq(f64(pool), 1, "e4m3") @ mxq(occ, 0, "e4m3")
    return track, load


def e4m3fn_bytes(y):
    return np.clip(np.asarray(y, np.float64), -448.0, 448.0).astype(np.float32).astype(ml_dtypes.float8_e4m3fn).view(np.uint8)


def e4m3fn_values(b):
    return np.asarray(b, np.uint8).view(ml_dtypes.float8_e4m3fn).astype(np.float64)


def setup_inputs():
    d = draw0()
    x0 = np.asarray(d['windows']).astype(np.float64)
    s = (np.max(np.abs(x0), axis=(0,), keepdims=True) / 448.0).astype(np.float32)
    out = {}
    for k, v in d.items():
        if k == 'windows':
            out['windows_bytes'] = e4m3fn_bytes(x0 / s.astype(np.float64))
            out['windows_scale'] = s
        else:
            out[k] = v
    return out


def reference(windows_bytes, windows_scale, motifs, access, activity, effects_words, effects_scales, pool):
    return core(e4m3fn_values(windows_bytes) * windows_scale.astype(np.float64), motifs, access, activity, effects_words, effects_scales, pool)

from contextlib import ExitStack

import concourse.mybir as mybir
from concourse.masks import make_identity

F32 = mybir.dt.float32
BF16 = mybir.dt.bfloat16
U32 = mybir.dt.uint32
I32 = mybir.dt.int32
U8 = mybir.dt.uint8
FP8 = mybir.dt.float8_e4m3fn
FP8X4 = mybir.dt.float8_e4m3fn_x4
FP4X4 = mybir.dt.float4_e2m1fn_x4
MULT = mybir.AluOpType.mult
ACT = mybir.ActivationFunctionType

N_POS, K_WIN, N_MOTIF, N_TRACK, N_REGION = 2048, 512, 1024, 512, 512
FLOPS = 2 * (N_POS * K_WIN * N_MOTIF + N_POS * N_MOTIF * N_TRACK + N_REGION * N_POS * N_MOTIF)

P = 128
GROUPS = 4
HALVES = 2
SLOTS = 4
W = 512
UNITS = ((0, 0), (1, 0), (0, 1), (2, 0), (3, 0), (1, 1), (2, 1), (3, 1))

ORDER = (
    (("prod", 0, 0,), "V"),
    (("prod", 0, 3,), "V"),
    (("prod", 0, 2,), "V"),
    (("mg", 0, 0,), "S"),
    (("mg", 0, 1,), "V"),
    (("wtr", 0, 1,), "P"),
    (("prod", 1, 2,), "V"),
    (("ap", 0,), "S"),
    (("prod", 1, 1,), "V"),
    (("wcp", 0, 1,), "S"),
    (("prod", 1, 3,), "V"),
    (("mg", 1, 0,), "S"),
    (("mq", 0,), "V"),
    (("wtr", 1, 1,), "P"),
    (("prod", 1, 0,), "V"),
    (("ptr", 0, 0,), "P"),
    (("wcp", 1, 1,), "S"),
    (("prod", 0, 1,), "V"),
    (("ptr", 0, 1,), "P"),
    (("pcp", 0, 0,), "S"),
    (("prod", 2, 2,), "V"),
    (("wtr", 1, 0,), "P"),
    (("pcp", 0, 1,), "S"),
    (("prod", 2, 3,), "V"),
    (("wtr", 0, 0,), "P"),
    (("wcp", 1, 0,), "S"),
    (("prod", 2, 0,), "V"),
    (("wtr", 2, 1,), "P"),
    (("wcp", 0, 0,), "S"),
    (("prod", 3, 1,), "V"),
    (("ptr", 1, 0,), "P"),
    (("wcp", 2, 1,), "S"),
    (("wq", 1,), "V"),
    (("ptr", 1, 1,), "P"),
    (("ap", 1,), "S"),
    (("prod", 3, 3,), "V"),
    (("ptr", 2, 1,), "P"),
    (("ptr", 2, 0,), "P"),
    (("prod", 2, 1,), "V"),
    (("pcp", 1, 1,), "S"),
    (("prod", 3, 2,), "V"),
    (("ptr", 3, 0,), "P"),
    (("pcp", 2, 1,), "S"),
    (("wtr", 2, 0,), "P"),
    (("wq", 0, 0,), "V"),
    (("pcp", 2, 0,), "S"),
    (("pq", 0,), "V"),
    (("ptr", 3, 1,), "P"),
    (("pcp", 3, 0,), "S"),
    (("pq", 2,), "V"),
    (("wtr", 3, 1,), "P"),
    (("wcp", 2, 0,), "S"),
    (("prod", 3, 0,), "V"),
    (("sc", 1,), "P"),
    (("wcp", 3, 1,), "S"),
    (("sc", 0,), "P"),
    (("wq", 2,), "V"),
    (("pcp", 3, 1,), "S"),
    (("wtr", 3, 0,), "P"),
    (("wq", 0, 1,), "V"),
    (("sig", 0,), "S"),
    (("mg", 1, 1,), "V"),
    (("sc", 4,), "P"),
    (("sc", 2,), "P"),
    (("sig", 1,), "S"),
    (("sc", 3,), "P"),
    (("stt", 0,), "V"),
    (("sc", 5,), "P"),
    (("sig", 2,), "S"),
    (("sc", 6,), "P"),
    (("stt", 1,), "V"),
    (("sc", 7,), "P"),
    (("sig", 3,), "S"),
    (("stt", 2,), "V"),
    (("otr", 0, 0,), "P"),
    (("sig", 4,), "S"),
    (("pq", 3,), "V"),
    (("sig", 5,), "S"),
    (("stt", 3,), "V"),
    (("sig", 6,), "S"),
    (("stt", 4,), "V"),
    (("otr", 0, 1,), "P"),
    (("rgB", 0,), "S"),
    (("rgA", 0,), "V"),
    (("ocp", 0, 1,), "S"),
    (("stt", 5,), "V"),
    (("pcp", 1, 0,), "S"),
    (("mq", 1,), "V"),
    (("ocp", 0, 0,), "S"),
    (("otr", 1, 0,), "P"),
    (("stt", 6,), "V"),
    (("wcp", 3, 0,), "S"),
    (("sc", 8,), "P"),
    (("sc", 9,), "P"),
    (("cq", 0,), "V"),
    (("sig", 7,), "S"),
    (("sc", 11,), "P"),
    (("sc", 10,), "P"),
    (("rq", 0,), "V"),
    (("sig", 8,), "S"),
    (("sc", 12,), "P"),
    (("sc", 13,), "P"),
    (("stt", 7,), "V"),
    (("sig", 9,), "S"),
    (("sc", 14,), "P"),
    (("stt", 8,), "V"),
    (("sig", 10,), "S"),
    (("otr", 1, 1,), "P"),
    (("sc", 15,), "P"),
    (("rgB", 1,), "V"),
    (("sig", 11,), "S"),
    (("stt", 9,), "V"),
    (("sig", 12,), "S"),
    (("rgA", 1,), "V"),
    (("otr", 2, 0,), "P"),
    (("sig", 13,), "S"),
    (("lm", 3, 0, 0,), "P"),
    (("sig", 14,), "S"),
    (("lm", 0, 0, 0,), "P"),
    (("stt", 10,), "V"),
    (("lm", 2, 0, 0,), "P"),
    (("sig", 15,), "S"),
    (("stt", 11,), "V"),
    (("ocp", 1, 1,), "S"),
    (("stt", 12,), "V"),
    (("otr", 2, 1,), "P"),
    (("rgB", 2,), "S"),
    (("lm", 1, 0, 0,), "P"),
    (("rgA", 2,), "V"),
    (("ocp", 2, 1,), "S"),
    (("stt", 13,), "V"),
    (("ocp", 2, 0,), "S"),
    (("stt", 14,), "V"),
    (("ocp", 1, 0,), "S"),
    (("otr", 3, 0,), "P"),
    (("cq", 2,), "V"),
    (("ocp", 3, 0,), "S"),
    (("cq", 1,), "V"),
    (("tm", 0, 1,), "P"),
    (("stt", 15,), "V"),
    (("tm", 0, 0,), "P"),
    (("to", 0, 1,), "S"),
    (("rq", 2,), "V"),
    (("tm", 0, 3,), "P"),
    (("to", 0, 0,), "S"),
    (("rgA", 3,), "V"),
    (("tm", 0, 2,), "P"),
    (("rgB", 3,), "S"),
    (("otr", 3, 1,), "P"),
    (("to", 0, 2,), "S"),
    (("wq", 3,), "V"),
    (("ocp", 3, 1,), "S"),
    (("rq", 3,), "V"),
    (("sc", 16,), "P"),
    (("to", 0, 3,), "S"),
    (("sc", 17,), "P"),
    (("cq", 3,), "V"),
    (("sc", 18,), "P"),
    (("sig", 16,), "S"),
    (("sc", 20,), "P"),
    (("pq", 1,), "V"),
    (("sig", 17,), "S"),
    (("sc", 19,), "P"),
    (("stt", 16,), "V"),
    (("sig", 18,), "S"),
    (("sc", 22,), "P"),
    (("stt", 17,), "V"),
    (("sig", 19,), "S"),
    (("sc", 21,), "P"),
    (("stt", 18,), "V"),
    (("sig", 20,), "S"),
    (("sc", 24,), "P"),
    (("stt", 19,), "V"),
    (("sig", 21,), "S"),
    (("sc", 25,), "P"),
    (("rq", 1,), "V"),
    (("sig", 22,), "S"),
    (("otr", 4, 1,), "P"),
    (("stt", 20,), "V"),
    (("lm", 3, 0, 1,), "P"),
    (("ocp", 4, 1,), "S"),
    (("stt", 21,), "V"),
    (("lm", 3, 0, 2,), "P"),
    (("sc", 26,), "P"),
    (("rgB", 4,), "S"),
    (("stt", 22,), "V"),
    (("sc", 23,), "P"),
    (("lm", 1, 0, 1,), "P"),
    (("sig", 23,), "S"),
    (("rgA", 4,), "V"),
    (("lm", 1, 0, 2,), "P"),
    (("lm", 0, 0, 1,), "P"),
    (("sig", 24,), "S"),
    (("sc", 27,), "P"),
    (("lm", 0, 0, 2,), "P"),
    (("sig", 25,), "S"),
    (("stt", 23,), "V"),
    (("sc", 29,), "P"),
    (("lm", 2, 0, 1,), "P"),
    (("sig", 26,), "S"),
    (("rq", 4,), "V"),
    (("sc", 30,), "P"),
    (("lm", 2, 0, 2,), "P"),
    (("sig", 27,), "S"),
    (("rgA", 5,), "V"),
    (("sc", 28,), "P"),
    (("lm", 3, 0, 3,), "P"),
    (("sig", 28,), "S"),
    (("lm", 1, 0, 3,), "P"),
    (("sc", 31,), "P"),
    (("lo", 3, 0,), "V"),
    (("sig", 29,), "S"),
    (("lm", 0, 0, 3,), "P"),
    (("lm", 2, 0, 3,), "P"),
    (("stt", 24,), "V"),
    (("lo", 1, 0,), "S"),
    (("lm", 3, 1, 0,), "P"),
    (("stt", 25,), "V"),
    (("otr", 4, 0,), "P"),
    (("sig", 30,), "S"),
    (("otr", 5, 1,), "P"),
    (("stt", 26,), "V"),
    (("sig", 31,), "S"),
    (("otr", 6, 0,), "P"),
    (("otr", 5, 0,), "P"),
    (("stt", 27,), "V"),
    (("ocp", 5, 1,), "S"),
    (("ocp", 5, 0,), "V"),
    (("otr", 6, 1,), "P"),
    (("rgB", 6,), "S"),
    (("lm", 0, 1, 0,), "P"),
    (("stt", 28,), "V"),
    (("ocp", 4, 0,), "S"),
    (("cq", 5,), "V"),
    (("ocp", 6, 1,), "S"),
    (("cq", 4,), "V"),
    (("tm", 1, 0,), "P"),
    (("ocp", 6, 0,), "S"),
    (("stt", 29,), "V"),
    (("tm", 1, 2,), "P"),
    (("rgB", 5,), "S"),
    (("cq", 6,), "V"),
    (("tm", 1, 1,), "P"),
    (("to", 1, 0,), "S"),
    (("rq", 5,), "V"),
    (("tm", 1, 3,), "P"),
    (("to", 1, 2,), "S"),
    (("stt", 30,), "V"),
    (("tm", 2, 3,), "P"),
    (("to", 1, 1,), "S"),
    (("rgA", 6,), "V"),
    (("lm", 3, 1, 1,), "P"),
    (("to", 1, 3,), "S"),
    (("lm", 0, 1, 1,), "P"),
    (("tm", 2, 2,), "P"),
    (("to", 2, 3,), "S"),
    (("stt", 31,), "V"),
    (("tm", 2, 1,), "P"),
    (("to", 2, 2,), "S"),
    (("rq", 6,), "V"),
    (("tm", 2, 0,), "P"),
    (("rgB", 7,), "S"),
    (("rgA", 7,), "V"),
    (("lm", 3, 1, 2,), "P"),
    (("lm", 0, 1, 2,), "P"),
    (("to", 2, 1,), "S"),
    (("otr", 7, 1,), "P"),
    (("to", 2, 0,), "S"),
    (("lo", 0, 0,), "V"),
    (("otr", 7, 0,), "P"),
    (("ocp", 7, 1,), "S"),
    (("rq", 7,), "V"),
    (("lm", 2, 1, 0,), "P"),
    (("lm", 2, 1, 1,), "P"),
    (("ocp", 7, 0,), "S"),
    (("lm", 2, 1, 2,), "P"),
    (("lo", 2, 0,), "V"),
    (("lm", 3, 1, 3,), "P"),
    (("lm", 2, 1, 3,), "P"),
    (("cq", 7, 1,), "V"),
    (("lo", 3, 1,), "S"),
    (("lm", 1, 1, 0,), "P"),
    (("cq", 7, 0,), "V"),
    (("lm", 1, 1, 1,), "P"),
    (("lo", 2, 1,), "V"),
    (("lm", 1, 1, 2,), "P"),
    (("lm", 0, 1, 3,), "P"),
    (("lm", 1, 1, 3,), "P"),
    (("lo", 0, 1,), "V"),
    (("tm", 3, 0,), "P"),
    (("lo", 1, 1,), "S"),
    (("tm", 3, 2,), "P"),
    (("to", 3, 0,), "V"),
    (("tm", 3, 1,), "P"),
    (("to", 3, 2,), "S"),
    (("tm", 3, 3,), "P"),
    (("to", 3, 1,), "V"),
    (("to", 3, 3,), "S"),
)


def tile_motif_scan_effects_s8_kernel(
    tc, windows_bytes, windows_scale, motifs, access, activity, effects_words, effects_scales, pool, track_out, load_out
):
    nc = tc.nc
    with ExitStack() as ctx:
        keep = ctx.enter_context(tc.tile_pool(name="keep", bufs=1))
        work = ctx.enter_context(tc.tile_pool(name="work", bufs=2))
        psum = ctx.enter_context(tc.psum_pool(name="psum", bufs=1))

        def kept(name, shape, dtype):
            return keep.tile(shape, dtype, name=name, tag=name, align_bytes=64)

        def worked(name, shape, dtype, bufs):
            return work.tile(shape, dtype, name=name, tag=name, bufs=bufs, align_bytes=64)

        def bank(b, shape):
            return psum.tile(shape, F32, name="bank%d" % b, tag="bank%d" % b)

        free_banks = list(range(8))
        used = {}

        def next_bank(role, shape):
            b = free_banks.pop(0)
            tile = bank(b, shape)
            return tile, b

        def release(b):
            free_banks.append(b)

        free_groups = ["grouped%d" % i for i in range(8)]
        group_slot = {}

        free_occ = ["occ%d" % i for i in range(3)]
        occ_slot = {}
        occ_reads = {}

        def occ_read(i):
            occ_reads[i] = occ_reads.get(i, 0) + 1
            if occ_reads[i] == 4:
                free_occ.append(occ_slot[i])

        def take_group(key):
            name = free_groups.pop(0)
            group_slot[key] = name
            return work.tile([P, 4 * W], BF16, name=name, tag=name, bufs=1, align_bytes=64)

        def give_group(key):
            free_groups.append(group_slot[key])

        scale_b = kept("scale_b", [P, K_WIN], F32)
        act_b = kept("act_b", [P, N_MOTIF], BF16)
        acc_sb = kept("acc_sb", [P, GROUPS, SLOTS], BF16)
        win_bytes = [kept("win_bytes%d" % g, [P, SLOTS, K_WIN], U8) for g in range(GROUPS)]
        motif_raw = [kept("motif_raw%d" % h, [P, 4, W], BF16) for h in range(HALVES)]
        pool_raw = [kept("pool_raw%d" % g, [P, 4, W], BF16) for g in range(GROUPS)]
        eff_words = kept("eff_words", [P, HALVES, 2 * N_TRACK], U8)
        eff_scales = kept("eff_scales", [P, HALVES, N_TRACK], U8)

        win_view = windows_bytes.rearrange("(g m t) k -> g m t k", g=GROUPS, t=SLOTS)
        motif_view = motifs.rearrange("(p j) (h c) -> h p j c", j=4, h=HALVES)
        pool_view = pool.rearrange("(a m) (g c) -> g m a c", a=4, g=GROUPS)

        nc.gpsimd.memset(eff_scales[:].bitcast(U32), 0)
        nc.scalar.dma_start(out=scale_b[:], in_=windows_scale.rearrange("o k -> (o k)").partition_broadcast(P))
        for b in range(2):
            nc.sync.dma_start(out=win_bytes[0][:, 2 * b : 2 * b + 2, :], in_=win_view[0][:, 2 * b : 2 * b + 2, :])
        nc.sync.dma_start(out=motif_raw[0][:], in_=motif_view[0])
        nc.sync.dma_start(out=win_bytes[1][:], in_=win_view[1])
        nc.scalar.dma_start(out=act_b[:], in_=activity.partition_broadcast(P))
        nc.scalar.dma_start(out=acc_sb[:], in_=access.rearrange("(g m t) -> m g t", g=GROUPS, t=SLOTS))
        nc.sync.dma_start(out=motif_raw[1][:], in_=motif_view[1])
        nc.sync.dma_start(out=pool_raw[0][:], in_=pool_view[0])
        nc.sync.dma_start(out=win_bytes[2][:], in_=win_view[2])
        nc.sync.dma_start(out=win_bytes[3][:], in_=win_view[3])
        nc.sync.dma_start(out=eff_words[:], in_=effects_words.rearrange("g p n -> p g n"))
        for g in range(1, GROUPS):
            nc.sync.dma_start(out=pool_raw[g][:], in_=pool_view[g])
        for q in range(4):
            nc.sync.dma_start(
                out=eff_scales[32 * q : 32 * q + 4].bitcast(I32),
                in_=effects_scales[:, 4 * q : 4 * q + 4, :].bitcast(I32).rearrange("g q n -> q g n"),
            )

        ident = kept("ident", [P, P], F32)
        make_identity(nc, ident[:])
        warm = kept("warm", [P, 8], F32)
        nc.gpsimd.memset(warm[:], 0.0)
        nc.scalar.activation(out=warm[:], in_=warm[:], func=ACT.Sigmoid)

        win_codes = kept("win_codes", [P, GROUPS, W], U32)
        win_scales = kept("win_scales", [P, GROUPS, W], U8)
        motif_codes = kept("motif_codes", [P, HALVES, W], U32)
        motif_scales = kept("motif_scales", [P, HALVES, W], U8)
        pool_codes = kept("pool_codes", [P, GROUPS, W], U32)
        pool_scales = kept("pool_scales", [P, GROUPS, W], U8)
        row_codes = kept("row_codes", [P, GROUPS, HALVES, W], U32)
        row_scales = kept("row_scales", [P, GROUPS, HALVES, W], U8)
        col_codes = kept("col_codes", [P, GROUPS, HALVES, W], U32)
        col_scales = kept("col_scales", [P, GROUPS, HALVES, W], U8)

        act_p = kept("act_p", [P, HALVES, W], BF16)
        win_bf = {}
        win_gr = {}
        pool_gr = {}
        motif_gr = {}
        occ = {}
        sig = {}
        score = {}
        occ_gr = {}
        row_gr = {}
        tr_tile = {}

        def act_order(u, eng):
            dst = act_p[:].rearrange("p h (u q e) -> p h u q e", u=2, e=2)[:, :, u]
            src = act_b[:].rearrange("p (h q u e) -> p h u q e", h=2, u=2, e=2)[:, :, u]
            if eng == "S":
                nc.scalar.copy(out=dst, in_=src)
            else:
                nc.vector.tensor_copy(out=dst, in_=src)

        def product(g, t):
            if g not in win_bf:
                win_bf[g] = worked("win_bf", [P, SLOTS, K_WIN], BF16, 4)
            nc.vector.tensor_tensor(
                out=win_bf[g][:, t, :], in0=win_bytes[g][:, t, :].bitcast(FP8), in1=scale_b[:], op=MULT
            )

        def transposes_even_words(key, words, b):
            tile, used[key] = next_bank("tr", [P, 2, 2, P])
            for s in range(2):
                for u in range(2):
                    nc.tensor.transpose(tile[:, s, u, :], words[:, 2 * b + s, u::2], ident[:])
            return tile

        def copy_words(eng, grouped, b, key):
            tile = tr_tile[key]
            release(used[key])
            dst = grouped[:].bitcast(F32)[:, b * W : (b + 1) * W].rearrange("p (s r u) -> p s r u", s=2, u=2)
            src = tile[:].rearrange("p s u r -> p s r u")
            if eng == "S":
                nc.scalar.copy(out=dst, in_=src)
            else:
                nc.vector.tensor_copy(out=dst, in_=src)

        def quantize(codes, scales, grouped):
            nc.vector.quantize_mx(out=codes.bitcast(FP8X4), scales=scales, in_=grouped)

        def win_tr(g, b):
            tr_tile["win", g, b] = transposes_even_words(("win", g, b), win_bf[g][:].bitcast(F32), b)

        def win_copy(g, b, eng):
            if g not in win_gr:
                win_gr[g] = take_group(("win", g))
            copy_words(eng, win_gr[g], b, ("win", g, b))

        def win_quant(g, b, parts):
            n = W // parts
            s = slice(b * n, (b + 1) * n)
            quantize(win_codes[:, g, s], win_scales[:, g, s], win_gr[g][:, 4 * b * n : 4 * (b + 1) * n])
            if b == parts - 1:
                give_group(("win", g))

        def pool_tr(g, b):
            tr_tile["pool", g, b] = transposes_even_words(("pool", g, b), pool_raw[g][:].bitcast(F32), b)

        def pool_copy(g, b, eng):
            if g not in pool_gr:
                pool_gr[g] = take_group(("pool", g))
            copy_words(eng, pool_gr[g], b, ("pool", g, b))

        def pool_quant(g):
            quantize(pool_codes[:, g, :], pool_scales[:, g, :], pool_gr[g][:])
            give_group(("pool", g))

        def motif_group(h, u, eng):
            if h not in motif_gr:
                motif_gr[h] = take_group(("motif", h))
            dst = motif_gr[h][:, u * 2 * W : (u + 1) * 2 * W].rearrange("p (q e j) -> p q e j", e=2, j=4)
            src = motif_raw[h][:].rearrange("p j (q u e) -> p u q e j", u=2, e=2)[:, u]
            if eng == "S":
                nc.scalar.copy(out=dst, in_=src)
            else:
                nc.vector.tensor_copy(out=dst, in_=src)

        def motif_quant(h):
            quantize(motif_codes[:, h, :], motif_scales[:, h, :], motif_gr[h][:])
            give_group(("motif", h))

        def scores(n):
            g, h = UNITS[n // 4]
            t = n % 4
            score[n], used["sc", n] = next_bank("score", [P, W])
            nc.tensor.matmul_mx(
                out=score[n][:],
                lhsT=win_codes[:, g, t * P : (t + 1) * P].bitcast(FP8X4),
                lhsT_scale=win_scales[:, g, t * P : (t + 1) * P],
                rhs=motif_codes[:, h, :].bitcast(FP8X4),
                rhs_scale=motif_scales[:, h, :],
                start=True,
                stop=True,
            )

        def sigmoid(n):
            sig[n] = worked("sig", [P, W], F32, 6)
            nc.scalar.activation(out=sig[n][:], in_=score[n][:], func=ACT.Sigmoid)
            release(used["sc", n])

        def occupancy(n):
            i, t = n // 4, n % 4
            g, h = UNITS[i]
            if i not in occ:
                occ_slot[i] = free_occ.pop(0)
                occ[i] = work.tile([P, SLOTS, W], BF16, name=occ_slot[i], tag=occ_slot[i], bufs=1, align_bytes=64)
            nc.vector.scalar_tensor_tensor(
                out=occ[i][:, t, :],
                in0=sig[n][:],
                scalar=acc_sb[:, g, t : t + 1],
                in1=act_p[:, h, :],
                op0=MULT,
                op1=MULT,
            )

        def occ_tr(i, b):
            words = occ[i][:].bitcast(F32)
            tile, used["occ", i, b] = next_bank("tr", [P, 2, 2, P])
            for s in range(2):
                for u in range(2):
                    nc.tensor.transpose(tile[:, s, u, :], words[:, 2 * b + s, u * P : (u + 1) * P], ident[:])
            tr_tile["occ", i, b] = tile
            occ_read(i)

        def occ_copy(i, b, eng):
            if i not in occ_gr:
                occ_gr[i] = take_group(("col", i))
            copy_words(eng, occ_gr[i], b, ("occ", i, b))

        def col_quant(i, b, parts):
            g, h = UNITS[i]
            n = W // parts
            s = slice(b * n, (b + 1) * n)
            quantize(col_codes[:, g, h, s], col_scales[:, g, h, s], occ_gr[i][:, 4 * b * n : 4 * (b + 1) * n])
            if b == parts - 1:
                give_group(("col", i))

        def row_group(i, c0, c1, eng):
            if i not in row_gr:
                row_gr[i] = take_group(("row", i))
            dst = row_gr[i][:, 4 * c0 : 4 * c1].rearrange("p (c i t) -> p c t i", i=4, t=4)
            src = occ[i][:, :, c0:c1].rearrange("p t (c i) -> p c t i", i=4)
            if eng == "S":
                nc.scalar.copy(out=dst, in_=src)
            else:
                nc.vector.tensor_copy(out=dst, in_=src)
            occ_read(i)

        def row_quant(i):
            g, h = UNITS[i]
            quantize(row_codes[:, g, h, :], row_scales[:, g, h, :], row_gr[i][:])
            give_group(("row", i))

        track_ps = {}
        load_ps = {}

        def track_mm(g, t):
            track_ps[g, t], used["track", g, t] = next_bank("out", [P, W])
            for h in range(HALVES):
                nc.tensor.matmul_mx(
                    out=track_ps[g, t][:],
                    lhsT=col_codes[:, g, h, t * P : (t + 1) * P].bitcast(FP8X4),
                    lhsT_scale=col_scales[:, g, h, t * P : (t + 1) * P],
                    rhs=eff_words[:, h, :].bitcast(FP4X4),
                    rhs_scale=eff_scales[:, h, :],
                    start=(h == 0),
                    stop=(h == HALVES - 1),
                )

        def track_copy(g, t, eng):
            release(used["track", g, t])
            sb = worked("track_sb", [P, N_TRACK], F32, 8)
            dst, src = sb[:], track_ps[g, t][:]
            if eng == "S":
                nc.scalar.copy(out=dst, in_=src)
            else:
                nc.vector.tensor_copy(out=dst, in_=src)
            nc.sync.dma_start(out=track_out.rearrange("(g m t) n -> g t m n", g=GROUPS, t=SLOTS)[g, t], in_=sb[:])

        def load_mm(a, h, k):
            if k == 0:
                load_ps[a, h], used["load", a, h] = next_bank("out", [P, W])
            g = [g for g, hh in UNITS if hh == h][k]
            nc.tensor.matmul_mx(
                out=load_ps[a, h][:],
                lhsT=pool_codes[:, g, a * P : (a + 1) * P].bitcast(FP8X4),
                lhsT_scale=pool_scales[:, g, a * P : (a + 1) * P],
                rhs=row_codes[:, g, h, :].bitcast(FP8X4),
                rhs_scale=row_scales[:, g, h, :],
                start=(k == 0),
                stop=(k == GROUPS - 1),
            )

        def load_copy(a, h, eng):
            release(used["load", a, h])
            sb = worked("load_sb", [P, W], F32, 6)
            dst = sb[:].rearrange("p (q u e) -> p q u e", u=2, e=2)
            src = load_ps[a, h][:].rearrange("p (u q e) -> p q u e", u=2, e=2)
            if eng == "S":
                nc.scalar.copy(out=dst, in_=src)
            else:
                nc.vector.tensor_copy(out=dst, in_=src)
            nc.sync.dma_start(out=load_out[a * P : (a + 1) * P, h * W : (h + 1) * W], in_=sb[:])

        with tc.manual_schedule():
            for step, eng in ORDER:
                kind, args = step[0], step[1:]
                if kind == "ap":
                    act_order(*args, eng)
                elif kind == "prod":
                    product(*args)
                elif kind == "wtr":
                    win_tr(*args)
                elif kind == "wcp":
                    win_copy(*args, eng)
                elif kind == "wq":
                    win_quant(args[0], args[1] if len(args) > 1 else 0, len(args))
                elif kind == "ptr":
                    pool_tr(*args)
                elif kind == "pcp":
                    pool_copy(*args, eng)
                elif kind == "pq":
                    pool_quant(*args)
                elif kind == "mg":
                    motif_group(*args, eng)
                elif kind == "mq":
                    motif_quant(*args)
                elif kind == "sc":
                    scores(*args)
                elif kind == "sig":
                    sigmoid(*args)
                elif kind == "stt":
                    occupancy(*args)
                elif kind == "otr":
                    occ_tr(*args)
                elif kind == "ocp":
                    occ_copy(*args, eng)
                elif kind == "cq":
                    col_quant(args[0], args[1] if len(args) > 1 else 0, len(args))
                elif kind == "rgA":
                    row_group(args[0], 0, 384, eng)
                elif kind == "rgB":
                    row_group(args[0], 384, W, eng)
                elif kind == "rq":
                    row_quant(*args)
                elif kind == "tm":
                    track_mm(*args)
                elif kind == "to":
                    track_copy(*args, eng)
                elif kind == "lm":
                    load_mm(*args)
                elif kind == "lo":
                    load_copy(*args, eng)
